import numpy as np
import ml_dtypes


def mxq(x, axis, fmt="e4m3"):
    dtype, down = {"e4m3": (ml_dtypes.float8_e4m3fn, 7), "e5m2": (ml_dtypes.float8_e5m2, 14)}[fmt]
    v = np.moveaxis(np.asarray(x, np.float32).astype(ml_dtypes.bfloat16).astype(np.float64), axis, -1)
    blocks = v.reshape(v.shape[:-1] + (-1, 32))
    amax = np.abs(blocks).max(-1, keepdims=True)
    byte = np.maximum(np.where(amax > 0, np.frexp(amax)[1] - 1 + 127, 0) - down, 1)
    scale = np.exp2(byte - 127.0)
    codes = (blocks / scale).astype(np.float32).astype(dtype).astype(np.float64)
    return np.moveaxis((codes * scale).reshape(v.shape), -1, axis)


WIDE = False


def mx_kscale(k):
    if not WIDE:
        return np.ones(k)
    levels = np.array([10, -10, 5, -5, 0])
    if k % 512:
        return np.exp2(np.random.permutation(np.resize(levels, k // 32))).repeat(32)
    a = np.empty((k // 512, 16))
    for p in range(k // 512):
        a[p, :8] = np.random.permutation(np.resize(levels, 8))
        for g in range(8):
            far = levels[np.abs(levels - a[p, g]) >= 10]
            a[p, g + 8] = far[np.random.randint(len(far))]
    return np.exp2(a.ravel()).repeat(32)


def f64(x):
    return np.asarray(x).astype(np.float64)


def striped(idx):
    return np.tile(np.asarray(idx).reshape(-1, 16).T, (8, 1)).astype(np.uint16)


def unstriped(offs):
    return offs[:16].T.reshape(-1).astype(np.int64)


E2M1 = np.array([0.0, 0.5, 1.0, 1.5, 2.0, 3.0, 4.0, 6.0, -0.0, -0.5, -1.0, -1.5, -2.0, -3.0, -4.0, -6.0])


def pack_weight(w, fmt):
    k, n = w.shape
    w = f64(np.asarray(w, np.float32).astype(ml_dtypes.bfloat16)).reshape(k // 32, 32, n)
    amax = np.abs(w).max(1)
    if fmt == "e4m3":
        byte = np.frexp(amax)[1] - 1 + 127 - 7
    else:
        mant, ex = np.frexp(amax / 6.0)
        byte = np.where(mant > 0.5, ex, ex - 1) + 127
    byte = np.clip(np.where(amax > 0, byte, 1), 1, 254)
    scaled = (w * np.exp2(127.0 - byte)[:, None, :]).reshape(k, n).astype(np.float32)
    by_word = np.ascontiguousarray(scaled.reshape(k // 512, 128, 4, n).transpose(0, 1, 3, 2))
    if fmt == "e4m3":
        words = by_word.astype(ml_dtypes.float8_e4m3fn).view(np.uint8)
    else:
        c = by_word.astype(ml_dtypes.float4_e2m1fn).view(np.uint8) & 0xF
        words = (c[..., 0::2] | (c[..., 1::2] << 4)).reshape(k // 512, 128, 2 * n)
    return np.ascontiguousarray(words), np.ascontiguousarray(byte.astype(np.uint8).reshape(k // 512, 16, n))


def unpack_weight(words, scales, fmt):
    g, _, n = scales.shape
    words = np.ascontiguousarray(words).reshape(g, 128, n, -1)
    if fmt == "e4m3":
        vals = words.view(ml_dtypes.float8_e4m3fn).astype(np.float64)
    else:
        nib = np.empty((g, 128, n, 4), np.uint8)
        nib[..., 0::2] = words & 0xF
        nib[..., 1::2] = words >> 4
        vals = E2M1[nib]
    vals = vals * np.repeat(np.exp2(scales.astype(np.float64) - 127.0), 8, axis=1)[..., None]
    return vals.transpose(0, 1, 3, 2).reshape(g * 512, n)


def silu(v):
    return v / (1.0 + np.exp(-v))


B, N, T, D, NQ = 1, 512, 4096, 1024, 128


def setup_inputs():
    n = np.random.standard_normal
    pages = np.random.permutation(T // 64)[:B * N // 64]
    idx = (pages[:, None] * 64 + np.arange(64)[None, :]).reshape(-1)
    s = mx_kscale(D)[:, None]
    kp = pack_weight(n((D, T)) / s, "e2m1")
    return {
        "qT": (n((B, D, NQ)) * s * (1.00 / np.sqrt(D))).astype(np.float32),
        "k_words": np.ascontiguousarray(kp[0].reshape(1, 2, 128, T, 2).transpose(0, 2, 3, 1, 4)).reshape(1, 128, T, 4),
        "k_scales": kp[1],
        "nb": np.tile(0.5 * n(4096), (128, 1)).astype(np.float32),
        "offs": striped(idx),
    }


def reference(qT, k_words, k_scales, nb, offs):
    idx = unstriped(offs)
    pick = lambda x, which: x[:, which].reshape(x.shape[0], B, -1).transpose(1, 0, 2)
    k = unpack_weight(k_words.reshape(1, 128, T, 2, 2).transpose(0, 3, 1, 2, 4).reshape(2, 128, 2 * T), k_scales, "e2m1")
    kg = pick(k, idx)
    qq = mxq(f64(qT), 1, "e4m3")
    a = qq.transpose(0, 2, 1) @ kg
    y = silu(a + pick(f64(nb), idx)[:, :1, :])
    return y

@@ -1,0 +1,137 @@
+from contextlib import ExitStack
+
+import concourse.mybir as mybir
+from concourse.masks import make_identity
+
+F32 = mybir.dt.float32
+BF16 = mybir.dt.bfloat16
+I32 = mybir.dt.int32
+U32 = mybir.dt.uint32
+U16 = mybir.dt.uint16
+U8 = mybir.dt.uint8
+FP8X4 = mybir.dt.float8_e4m3fn_x4
+FP4X4 = mybir.dt.float4_e2m1fn_x4
+SILU = mybir.ActivationFunctionType.Silu
+ADD = mybir.AluOpType.add
+
+P = 128
+T = 4096
+N = 512
+D = 1024
+NQ = 128
+PACK = 4
+K_PASS = P * PACK
+PASSES = D // K_PASS
+GROUP = 128
+GROUPS = N // GROUP
+SCALE_ROWS = 16
+QUADS = 4
+ROWS_PER_QUAD = SCALE_ROWS // QUADS
+SCALE_BASE = P - PASSES * SCALE_ROWS
+NB_ROW = P - 1
+
+FLOPS = 2 * NQ * N * D
+BYTES = 4 * D * NQ + P * T * 4 + PASSES * SCALE_ROWS * T + 4 * T + 2 * P * (N // 16) + 4 * NQ * N
+
+
+def tile_attend_neu_block_kernel(tc, qT, k_words, k_scales, nb, offs, out):
+    nc = tc.nc
+    with ExitStack() as ctx:
+        keep = ctx.enter_context(tc.tile_pool(name="keep", bufs=1))
+        psum = ctx.enter_context(tc.psum_pool(name="psum", bufs=1))
+
+        offsets = keep.tile([P, N // 16], U16, name="offsets")
+        nc.sync.dma_start(offsets[:], offs)
+
+        nb_win = keep.tile([P, T], F32, name="nb_win")
+        nc.scalar.dma_start(out=nb_win[NB_ROW:P, :], in_=nb[0:1, :])
+        scale_win = keep.tile([P, T], U8, name="scale_win")
+        nc.scalar.dma_start(
+            out=scale_win[SCALE_BASE:P, :].bitcast(I32),
+            in_=k_scales.bitcast(I32).rearrange("o f t -> f o t"),
+        )
+
+        word_win = keep.tile([P, T], I32, name="word_win")
+        nc.sync.dma_start(out=word_win[:], in_=k_words[0].rearrange("p t b -> p (t b)").bitcast(I32))
+        q_raw = []
+        for o in range(PASSES):
+            raw = keep.tile([P, PACK, NQ], F32, name="q_raw%d" % o)
+            nc.sync.dma_start(
+                out=raw[:],
+                in_=qT[0, o * K_PASS : (o + 1) * K_PASS, :].rearrange("(p t) q -> p t q", t=PACK),
+            )
+            q_raw.append(raw)
+
+        zero = keep.tile([P, 2], F32, name="zero")
+        nc.gpsimd.memset(zero[:], 0.0)
+        no_bias = keep.tile([P, 2], F32, name="no_bias")
+        nc.scalar.activation(no_bias[:], zero[:], SILU)
+
+        ident = keep.tile([P, P], F32, name="ident")
+        make_identity(nc, ident[:])
+        k_planes = keep.tile([P, PASSES, N], U8, name="k_planes", align_bytes=64)
+        nc.gpsimd.memset(k_planes[:].bitcast(I32), 0)
+
+        nc.vector.memset(scale_win[0:SCALE_BASE, :].bitcast(I32), 0)
+        nc.vector.memset(nb_win[0:NB_ROW, :], 0.0)
+
+        scale_got = keep.tile([P, N], U8, name="scale_got")
+        nc.vector.tensor_copy(scale_got[:], scale_win[:].indirect(offsets[:]))
+        for quad in range(QUADS):
+            first = SCALE_BASE + quad * ROWS_PER_QUAD * PASSES
+            nc.scalar.dma_start(
+                out=k_planes[32 * quad : 32 * quad + ROWS_PER_QUAD, :, :].bitcast(I32),
+                in_=scale_got[first : first + ROWS_PER_QUAD * PASSES, :].bitcast(I32),
+            )
+
+        nb_got = keep.tile([P, N], F32, name="nb_got")
+        nc.vector.tensor_copy(nb_got[:], nb_win[:].indirect(offsets[:]))
+        turned = psum.tile([P, GROUPS, GROUP], F32, name="turned")
+        for j in range(GROUPS):
+            nc.tensor.transpose(turned[:, j, :], nb_got[:, j * GROUP : (j + 1) * GROUP], ident[:])
+        nb_cols = keep.tile([P, GROUPS], F32, name="nb_cols")
+        nc.scalar.copy(nb_cols[:], turned[:, :, NB_ROW])
+        spread = psum.tile([P, GROUPS, GROUP], F32, name="spread")
+        for j in range(GROUPS):
+            nc.tensor.transpose(spread[:, j, :], nb_cols[:, j : j + 1].to_broadcast([P, P]), ident[:])
+        bias = keep.tile([P, GROUPS, GROUP], F32, name="bias")
+        nc.scalar.copy(bias[:], spread[:])
+
+        word_got = keep.tile([P, N], U32, name="word_got")
+        nc.vector.tensor_copy(word_got[:], word_win[:].bitcast(U32).indirect(offsets[:]))
+        halves = word_got[:].bitcast(U16).rearrange("p (n o) -> p o n", o=PASSES)
+
+        acc = [psum.tile([NQ, GROUP], F32, name="acc%d" % j) for j in range(GROUPS)]
+        for o in range(PASSES):
+            k_codes = keep.tile([P, 2 * N], U8, name="k_codes%d" % o, align_bytes=64)
+            nc.vector.tensor_copy(k_codes[:].bitcast(U16), halves[:, o, :])
+
+            q_bf = keep.tile([P, NQ, PACK], BF16, name="q_bf%d" % o, align_bytes=64)
+            nc.scalar.copy(
+                q_bf[:].rearrange("p (c i) t -> p c t i", i=4),
+                q_raw[o][:].rearrange("p t (c i) -> p c t i", i=4),
+            )
+            q_codes = keep.tile([P, NQ], U32, name="q_codes%d" % o, align_bytes=64)
+            q_scales = keep.tile([P, NQ], U8, name="q_scales%d" % o, align_bytes=64)
+            nc.vector.quantize_mx(
+                out=q_codes[:].bitcast(FP8X4),
+                scales=q_scales[:],
+                in_=q_bf[:].rearrange("p q t -> p (q t)"),
+            )
+            for j in range(GROUPS):
+                nc.tensor.matmul_mx(
+                    out=acc[j][:],
+                    lhsT=q_codes[:].bitcast(FP8X4),
+                    lhsT_scale=q_scales[:],
+                    rhs=k_codes[:, 2 * j * GROUP : 2 * (j + 1) * GROUP].bitcast(FP4X4),
+                    rhs_scale=k_planes[:, o, j * GROUP : (j + 1) * GROUP],
+                    start=(o == 0),
+                    stop=(o == PASSES - 1),
+                )
+
+        for j in range(GROUPS):
+            pre = keep.tile([NQ, GROUP], F32, name="pre%d" % j)
+            nc.vector.tensor_tensor(pre[:], acc[j][:], bias[:, j, :], ADD)
+            y = keep.tile([NQ, GROUP], F32, name="y%d" % j)
+            nc.scalar.activation(y[:], pre[:], SILU, bias=no_bias[:, 0:1])
+            nc.sync.dma_start(out=out[0, :, j * GROUP : (j + 1) * GROUP], in_=y[:])

@@ -43,9 +43,9 @@ def tile_attend_neu_block_kernel(tc, qT, k_words, k_scales, nb, offs, out):
         offsets = keep.tile([P, N // 16], U16, name="offsets")
         nc.sync.dma_start(offsets[:], offs)
 
-        nb_win = keep.tile([P, T], F32, name="nb_win")
-        nc.scalar.dma_start(out=nb_win[NB_ROW:P, :], in_=nb[0:1, :])
-        scale_win = keep.tile([P, T], U8, name="scale_win")
+        nb_win = keep.tile([P, T], F32, name="nb_win", tag="nb_then_words")
+        nc.sync.dma_start(out=nb_win[NB_ROW:P, :], in_=nb[0:1, :])
+        scale_win = keep.tile([P, T], U8, name="scale_win", tag="scales_then_nb")
         nc.scalar.dma_start(
             out=scale_win[SCALE_BASE:P, :].bitcast(I32),
             in_=k_scales.bitcast(I32).rearrange("o f t -> f o t"),
@@ -55,7 +55,7 @@ def tile_attend_neu_block_kernel(tc, qT, k_words, k_scales, nb, offs, out):
         nc.sync.dma_start(out=word_win[:], in_=k_words[0].rearrange("p t b -> p (t b)").bitcast(I32))
         q_raw = []
         for o in range(PASSES):
-            raw = keep.tile([P, PACK, NQ], F32, name="q_raw%d" % o)
+            raw = keep.tile([P, PACK, NQ], F32, name="q_raw%d" % o, tag="q_raw%d" % o)
             nc.sync.dma_start(
                 out=raw[:],
                 in_=qT[0, o * K_PASS : (o + 1) * K_PASS, :].rearrange("(p t) q -> p t q", t=PACK),
@@ -84,7 +84,7 @@ def tile_attend_neu_block_kernel(tc, qT, k_words, k_scales, nb, offs, out):
                 in_=scale_got[first : first + ROWS_PER_QUAD * PASSES, :].bitcast(I32),
             )
 
-        nb_got = keep.tile([P, N], F32, name="nb_got")
+        nb_got = keep.tile([P, N], F32, name="nb_got", tag="scales_then_nb")
         nc.vector.tensor_copy(nb_got[:], nb_win[:].indirect(offsets[:]))
         turned = psum.tile([P, GROUPS, GROUP], F32, name="turned")
         for j in range(GROUPS):
@@ -94,10 +94,8 @@ def tile_attend_neu_block_kernel(tc, qT, k_words, k_scales, nb, offs, out):
         spread = psum.tile([P, GROUPS, GROUP], F32, name="spread")
         for j in range(GROUPS):
             nc.tensor.transpose(spread[:, j, :], nb_cols[:, j : j + 1].to_broadcast([P, P]), ident[:])
-        bias = keep.tile([P, GROUPS, GROUP], F32, name="bias")
-        nc.scalar.copy(bias[:], spread[:])
 
-        word_got = keep.tile([P, N], U32, name="word_got")
+        word_got = keep.tile([P, N], U32, name="word_got", tag="nb_then_words")
         nc.vector.tensor_copy(word_got[:], word_win[:].bitcast(U32).indirect(offsets[:]))
         halves = word_got[:].bitcast(U16).rearrange("p (n o) -> p o n", o=PASSES)
 
@@ -129,6 +127,8 @@ def tile_attend_neu_block_kernel(tc, qT, k_words, k_scales, nb, offs, out):
                     stop=(o == PASSES - 1),
                 )
 
+        bias = keep.tile([P, GROUPS, GROUP], F32, name="bias", tag="q_raw%d" % (PASSES - 1))
+        nc.scalar.copy(bias[:], spread[:])
         for j in range(GROUPS):
             pre = keep.tile([NQ, GROUP], F32, name="pre%d" % j)
             nc.vector.tensor_tensor(pre[:], acc[j][:], bias[:, j, :], ADD)

from contextlib import ExitStack

import concourse.mybir as mybir
from concourse.masks import make_identity

F32 = mybir.dt.float32
BF16 = mybir.dt.bfloat16
I32 = mybir.dt.int32
U32 = mybir.dt.uint32
U16 = mybir.dt.uint16
U8 = mybir.dt.uint8
FP8X4 = mybir.dt.float8_e4m3fn_x4
FP4X4 = mybir.dt.float4_e2m1fn_x4
SILU = mybir.ActivationFunctionType.Silu
ADD = mybir.AluOpType.add

P = 128
T = 4096
N = 512
D = 1024
NQ = 128
PACK = 4
K_PASS = P * PACK
PASSES = D // K_PASS
GROUP = 128
GROUPS = N // GROUP
SCALE_ROWS = 16
QUADS = 4
ROWS_PER_QUAD = SCALE_ROWS // QUADS
SCALE_BASE = P - PASSES * SCALE_ROWS
NB_ROW = P - 1

FLOPS = 2 * NQ * N * D
BYTES = 4 * D * NQ + P * T * 4 + PASSES * SCALE_ROWS * T + 4 * T + 2 * P * (N // 16) + 4 * NQ * N


def tile_attend_neu_block_kernel(tc, qT, k_words, k_scales, nb, offs, out):
    nc = tc.nc
    with ExitStack() as ctx:
        keep = ctx.enter_context(tc.tile_pool(name="keep", bufs=1))
        psum = ctx.enter_context(tc.psum_pool(name="psum", bufs=1))

        offsets = keep.tile([P, N // 16], U16, name="offsets")
        nc.sync.dma_start(offsets[:], offs)

        nb_win = keep.tile([P, T], F32, name="nb_win", tag="nb_then_words")
        nc.sync.dma_start(out=nb_win[NB_ROW:P, :], in_=nb[0:1, :])
        scale_win = keep.tile([P, T], U8, name="scale_win", tag="scales_then_nb")
        nc.scalar.dma_start(
            out=scale_win[SCALE_BASE:P, :].bitcast(I32),
            in_=k_scales.bitcast(I32).rearrange("o f t -> f o t"),
        )

        word_win = keep.tile([P, T], I32, name="word_win")
        nc.sync.dma_start(out=word_win[:], in_=k_words[0].rearrange("p t b -> p (t b)").bitcast(I32))
        q_raw = []
        for o in range(PASSES):
            raw = keep.tile([P, PACK, NQ], F32, name="q_raw%d" % o, tag="q_raw%d" % o)
            nc.sync.dma_start(
                out=raw[:],
                in_=qT[0, o * K_PASS : (o + 1) * K_PASS, :].rearrange("(p t) q -> p t q", t=PACK),
            )
            q_raw.append(raw)

        zero = keep.tile([P, 2], F32, name="zero")
        nc.gpsimd.memset(zero[:], 0.0)
        no_bias = keep.tile([P, 2], F32, name="no_bias")
        nc.scalar.activation(no_bias[:], zero[:], SILU)

        ident = keep.tile([P, P], F32, name="ident")
        make_identity(nc, ident[:])
        k_planes = keep.tile([P, PASSES, N], U8, name="k_planes", align_bytes=64)
        nc.gpsimd.memset(k_planes[:].bitcast(I32), 0)

        nc.vector.memset(scale_win[0:SCALE_BASE, :].bitcast(I32), 0)
        nc.vector.memset(nb_win[0:NB_ROW, :], 0.0)

        scale_got = keep.tile([P, N], U8, name="scale_got")
        nc.vector.tensor_copy(scale_got[:], scale_win[:].indirect(offsets[:]))
        for quad in range(QUADS):
            first = SCALE_BASE + quad * ROWS_PER_QUAD * PASSES
            nc.scalar.dma_start(
                out=k_planes[32 * quad : 32 * quad + ROWS_PER_QUAD, :, :].bitcast(I32),
                in_=scale_got[first : first + ROWS_PER_QUAD * PASSES, :].bitcast(I32),
            )

        nb_got = keep.tile([P, N], F32, name="nb_got", tag="scales_then_nb")
        nc.vector.tensor_copy(nb_got[:], nb_win[:].indirect(offsets[:]))
        turned = psum.tile([P, GROUPS, GROUP], F32, name="turned")
        for j in range(GROUPS):
            nc.tensor.transpose(turned[:, j, :], nb_got[:, j * GROUP : (j + 1) * GROUP], ident[:])
        nb_cols = keep.tile([P, GROUPS], F32, name="nb_cols")
        nc.scalar.copy(nb_cols[:], turned[:, :, NB_ROW])
        spread = psum.tile([P, GROUPS, GROUP], F32, name="spread")
        for j in range(GROUPS):
            nc.tensor.transpose(spread[:, j, :], nb_cols[:, j : j + 1].to_broadcast([P, P]), ident[:])

        word_got = keep.tile([P, N], U32, name="word_got", tag="nb_then_words")
        nc.vector.tensor_copy(word_got[:], word_win[:].bitcast(U32).indirect(offsets[:]))
        halves = word_got[:].bitcast(U16).rearrange("p (n o) -> p o n", o=PASSES)

        acc = [psum.tile([NQ, GROUP], F32, name="acc%d" % j) for j in range(GROUPS)]
        for o in range(PASSES):
            k_codes = keep.tile([P, 2 * N], U8, name="k_codes%d" % o, align_bytes=64)
            nc.vector.tensor_copy(k_codes[:].bitcast(U16), halves[:, o, :])

            q_bf = keep.tile([P, NQ, PACK], BF16, name="q_bf%d" % o, align_bytes=64)
            nc.scalar.copy(
                q_bf[:].rearrange("p (c i) t -> p c t i", i=4),
                q_raw[o][:].rearrange("p t (c i) -> p c t i", i=4),
            )
            q_codes = keep.tile([P, NQ], U32, name="q_codes%d" % o, align_bytes=64)
            q_scales = keep.tile([P, NQ], U8, name="q_scales%d" % o, align_bytes=64)
            nc.vector.quantize_mx(
                out=q_codes[:].bitcast(FP8X4),
                scales=q_scales[:],
                in_=q_bf[:].rearrange("p q t -> p (q t)"),
            )
            for j in range(GROUPS):
                nc.tensor.matmul_mx(
                    out=acc[j][:],
                    lhsT=q_codes[:].bitcast(FP8X4),
                    lhsT_scale=q_scales[:],
                    rhs=k_codes[:, 2 * j * GROUP : 2 * (j + 1) * GROUP].bitcast(FP4X4),
                    rhs_scale=k_planes[:, o, j * GROUP : (j + 1) * GROUP],
                    start=(o == 0),
                    stop=(o == PASSES - 1),
                )

        bias = keep.tile([P, GROUPS, GROUP], F32, name="bias", tag="q_raw%d" % (PASSES - 1))
        nc.scalar.copy(bias[:], spread[:])
        for j in range(GROUPS):
            pre = keep.tile([NQ, GROUP], F32, name="pre%d" % j)
            nc.vector.tensor_tensor(pre[:], acc[j][:], bias[:, j, :], ADD)
            y = keep.tile([NQ, GROUP], F32, name="y%d" % j)
            nc.scalar.activation(y[:], pre[:], SILU, bias=no_bias[:, 0:1])
            nc.sync.dma_start(out=out[0, :, j * GROUP : (j + 1) * GROUP], in_=y[:])
